import numpy as np
import ml_dtypes


def mxq(x, axis, fmt="e4m3"):
    dtype, down = {"e4m3": (ml_dtypes.float8_e4m3fn, 7), "e5m2": (ml_dtypes.float8_e5m2, 14)}[fmt]
    v = np.moveaxis(np.asarray(x, np.float32).astype(ml_dtypes.bfloat16).astype(np.float64), axis, -1)
    blocks = v.reshape(v.shape[:-1] + (-1, 32))
    amax = np.abs(blocks).max(-1, keepdims=True)
    byte = np.maximum(np.where(amax > 0, np.frexp(amax)[1] - 1 + 127, 0) - down, 1)
    scale = np.exp2(byte - 127.0)
    codes = (blocks / scale).astype(np.float32).astype(dtype).astype(np.float64)
    return np.moveaxis((codes * scale).reshape(v.shape), -1, axis)


WIDE = False


def mx_kscale(k):
    if not WIDE:
        return np.ones(k)
    levels = np.array([10, -10, 5, -5, 0])
    if k % 512:
        return np.exp2(np.random.permutation(np.resize(levels, k // 32))).repeat(32)
    a = np.empty((k // 512, 16))
    for p in range(k // 512):
        a[p, :8] = np.random.permutation(np.resize(levels, 8))
        for g in range(8):
            far = levels[np.abs(levels - a[p, g]) >= 10]
            a[p, g + 8] = far[np.random.randint(len(far))]
    return np.exp2(a.ravel()).repeat(32)


def f64(x):
    return np.asarray(x).astype(np.float64)


def striped(idx):
    return np.tile(idx.reshape(-1, 16).T, (8, 1)).astype(np.uint16)


def unstriped(offs):
    return offs[:16].T.reshape(-1).astype(np.int64)


def striped8(idx):
    return np.concatenate([x.reshape(-1, 16).T for x in idx]).astype(np.uint16)


def runs(offs, k):
    lists = np.stack([offs[16 * r : 16 * r + 16].T.reshape(-1) for r in range(8)]).astype(np.int64)
    return lists[np.arange(k) % 512 // 64]


def pack_weight(w):
    k, n = w.shape
    w = f64(np.asarray(w, np.float32).astype(ml_dtypes.bfloat16)).reshape(k // 32, 32, n)
    amax = np.abs(w).max(1)
    byte = np.clip(np.where(amax > 0, np.frexp(amax)[1] - 1 + 127 - 7, 1), 1, 254)
    scaled = (w * np.exp2(127.0 - byte)[:, None, :]).reshape(k, n).astype(np.float32)
    words = np.ascontiguousarray(scaled.reshape(k // 512, 128, 4, n).transpose(0, 1, 3, 2)).astype(ml_dtypes.float8_e4m3fn).view(np.uint8)
    return words, np.ascontiguousarray(byte.astype(np.uint8).reshape(k // 512, 16, n))


def unpack_weight(words, scales):
    g, p, n, _ = words.shape
    vals = np.ascontiguousarray(words).view(ml_dtypes.float8_e4m3fn).astype(np.float64) * np.repeat(np.exp2(scales.astype(np.float64) - 127.0), 8, axis=1)[..., None]
    return vals.transpose(0, 1, 3, 2).reshape(g * 512, n)


def relu(v):
    return np.maximum(v, 0.0)


K, T, S, H, G = 512, 2048, 512, 512, 2048


def setup_inputs():
    n = np.random.standard_normal
    s = mx_kscale(K)[:, None]
    packed_xT = pack_weight(n((K, T)) * s)
    packed_dT = pack_weight(n((K, G)) / s)
    return {
        "x_words": packed_xT[0],
        "x_scales": packed_xT[1],
        "w1": (n((K, H)) / np.sqrt(K) / s).astype(np.float32),
        "gs": (np.random.uniform(0.5, 1.5, (K, 1)) * s).astype(np.float32),
        "d_words": packed_dT[0],
        "d_scales": packed_dT[1],
        "offs": striped(np.random.permutation(T)[:S]),
        "n1": striped8(np.stack([np.random.permutation(S) for _ in range(8)])),
        "n2": striped8(np.stack([np.random.permutation(S) for _ in range(8)])),
        "k1": striped8(np.random.randint(0, G, (8, H))),
        "n3": striped8(np.stack([np.random.permutation(S) for _ in range(8)])),
        "n4": striped8(np.stack([np.random.permutation(S) for _ in range(8)])),
    }


def reference(x_words, x_scales, w1, gs, d_words, d_scales, offs, n1, n2, k1, n3, n4):
    d_k1 = unpack_weight(d_words, d_scales)[np.arange(K)[:, None], runs(k1, K)]
    xq = unpack_weight(x_words, x_scales)[:, unstriped(offs)]
    y = mxq(f64(w1), 0, "e4m3").T @ xq
    pa = y - (y[np.arange(H)[:, None], runs(n1, H)])
    pb = y[np.arange(H)[:, None], runs(n2, H)] - y
    z = f64(gs) * (relu(np.minimum(pa, pb)) - (relu(-1.0 * np.maximum(pa, pb))))
    h = 0.0625 * ((d_k1.T @ mxq(z, 0, "e4m3")))
    return np.maximum(h[np.arange(H)[:, None], runs(n3, H)], h[np.arange(H)[:, None], runs(n4, H)]) - (0.75 * h)

@@ -1,0 +1,196 @@
+from contextlib import ExitStack
+
+import concourse.mybir as mybir
+
+K, T, S, H, G = 512, 2048, 512, 512, 2048
+FLOPS = 2 * 2 * K * H * S
+
+F32 = mybir.dt.float32
+BF16 = mybir.dt.bfloat16
+I32 = mybir.dt.int32
+U32 = mybir.dt.uint32
+U16 = mybir.dt.uint16
+U8 = mybir.dt.uint8
+FP8X4 = mybir.dt.float8_e4m3fn_x4
+ALU = mybir.AluOpType
+COPY = mybir.ActivationFunctionType.Copy
+
+P = 128
+PACK = 4
+CHUNKS = ((0, 256), (256, 384), (384, 512))
+HALVES = ((0, 256), (256, 512))
+
+
+def tile_picked_denseminmodover_none_p_kernel(
+    tc, x_words, x_scales, w1, gs, d_words, d_scales, offs, n1, n2, k1, n3, n4, out
+):
+    nc = tc.nc
+    with ExitStack() as ctx:
+        lists = ctx.enter_context(tc.tile_pool(name="lists", bufs=1))
+        keep = ctx.enter_context(tc.tile_pool(name="keep", bufs=1))
+        psum = ctx.enter_context(tc.psum_pool(name="psum", bufs=1))
+
+        def list_tile(name):
+            return lists.tile([P, S // 16], U16, name=name)
+
+        def entries(tile, c0, c1):
+            return tile[:, c0 // 16 : c1 // 16]
+
+        offs_sb, n1_sb, n2_sb = list_tile("offs_sb"), list_tile("n1_sb"), list_tile("n2_sb")
+        k1_sb, n3_sb, n4_sb = list_tile("k1_sb"), list_tile("n3_sb"), list_tile("n4_sb")
+
+        x_scale_table = keep.tile([P, T], U8, name="x_scale_table")
+        d_scale_table = keep.tile([P, G], U8, name="d_scale_table")
+        d_scale_plane = keep.tile([P, H], U8, name="d_scale_plane", align_bytes=64)
+        x_word_table = keep.tile([P, T], U32, name="x_word_table")
+        d_word_table = keep.tile([P, G], U32, name="d_word_table")
+        w_raw = [keep.tile([P, PACK, H // 2], F32, name=f"w_raw{u}") for u in range(2)]
+        gs_sb = keep.tile([P, PACK], F32, name="gs_sb")
+        gs_neg = keep.tile([P, PACK], F32, name="gs_neg")
+
+        nc.vector.memset(x_scale_table[:].bitcast(I32), 0)
+        nc.gpsimd.memset(d_scale_table[:].bitcast(I32), 0)
+
+        w_rows = w1.rearrange("(p j) c -> p j c", j=PACK)
+        nc.sync.dma_start(offs_sb[:], offs)
+        nc.sync.dma_start(x_word_table[:].bitcast(I32), x_words[0].rearrange("p n t -> p (n t)").bitcast(I32))
+        for q in range(4):
+            nc.scalar.dma_start(
+                x_scale_table[32 * q : 32 * q + 4, :].bitcast(I32), x_scales[0, 4 * q : 4 * q + 4, :].bitcast(I32)
+            )
+        for u in range(2):
+            nc.sync.dma_start(w_raw[u][:], w_rows[:, :, u * (H // 2) : (u + 1) * (H // 2)])
+        d_scale_rows = d_scales[0].rearrange("(q r) n -> r q n", r=4)
+        for r in range(4):
+            first = 16 * (r // 2) + r % 2
+            nc.gpsimd.dma_start(d_scale_table[first:P:32, :].bitcast(I32), d_scale_rows[r].bitcast(I32))
+        nc.gpsimd.memset(d_scale_plane[:].bitcast(I32), 0)
+        nc.sync.dma_start(gs_sb[:], gs.rearrange("(p t) o -> p (t o)", t=PACK))
+        nc.sync.dma_start(k1_sb[:], k1)
+        nc.sync.dma_start(n1_sb[:], n1)
+        nc.sync.dma_start(n2_sb[:], n2)
+        nc.sync.dma_start(d_word_table[:].bitcast(I32), d_words[0].rearrange("p n t -> p (n t)").bitcast(I32))
+        nc.sync.dma_start(n3_sb[:], n3)
+        nc.sync.dma_start(n4_sb[:], n4)
+
+        nc.scalar.activation(gs_neg[:], gs_sb[:], COPY, scale=-1.0)
+
+        x_scale_picked = keep.tile([P, S], U8, name="x_scale_picked", align_bytes=64)
+        x_word_picked = keep.tile([P, S], U32, name="x_word_picked", align_bytes=64)
+        nc.vector.tensor_copy(x_scale_picked[:], x_scale_table[:].indirect(offs_sb[:]))
+        nc.vector.tensor_copy(x_word_picked[:], x_word_table[:].indirect(offs_sb[:]))
+
+        w_grouped = keep.tile([P, PACK, P, PACK], BF16, name="w_grouped", align_bytes=64)
+        for u, copy in enumerate((nc.scalar.copy, nc.vector.tensor_copy)):
+            copy(
+                w_grouped[:, :, u * (P // 2) : (u + 1) * (P // 2), :].rearrange("p t m j -> p m j t"),
+                w_raw[u][:].rearrange("p j (m t) -> p m j t", t=PACK),
+            )
+
+        y_pos, y_neg = [], []
+        for t in range(PACK):
+            w_words = keep.tile([P, P], U32, name=f"w_words{t}", align_bytes=64)
+            w_scales = keep.tile([P, P], U8, name=f"w_scales{t}", align_bytes=64)
+            nc.vector.quantize_mx(
+                out=w_words[:].bitcast(FP8X4), scales=w_scales[:], in_=w_grouped[:, t].rearrange("p m j -> p (m j)")
+            )
+            y_bank = psum.tile([P, S], F32, name=f"y_bank{t}")
+            nc.tensor.matmul_mx(
+                out=y_bank[:],
+                lhsT=w_words[:].bitcast(FP8X4),
+                lhsT_scale=w_scales[:],
+                rhs=x_word_picked[:].bitcast(FP8X4),
+                rhs_scale=x_scale_picked[:],
+                start=True,
+                stop=True,
+            )
+            y_pos.append(keep.tile([P, S], F32, name=f"y_pos{t}"))
+            y_neg.append(keep.tile([P, S], F32, name=f"y_neg{t}"))
+            nc.scalar.activation(y_pos[t][:], y_bank[:], COPY, scale=gs_sb[:, t : t + 1])
+            nc.scalar.activation(y_neg[t][:], y_bank[:], COPY, scale=gs_neg[:, t : t + 1])
+
+        d_scale_picked = keep.tile([P, H], U8, name="d_scale_picked")
+        d_scale_dealt = keep.tile([P, PACK, P], U8, name="d_scale_dealt")
+        nc.vector.tensor_copy(d_scale_picked[:], d_scale_table[:].indirect(k1_sb[:]))
+        nc.vector.tensor_copy(
+            d_scale_dealt[:].rearrange("p t m -> p m t"), d_scale_picked[:].rearrange("p (m t) -> p m t", t=PACK)
+        )
+        for r in range(4):
+            first = 16 * (r // 2) + r % 2
+            nc.sync.dma_start(
+                d_scale_plane[r:P:32, :].bitcast(I32),
+                d_scale_dealt[first:P:32].rearrange("p t m -> p (t m)").bitcast(I32),
+            )
+
+        def differences(c0, c1):
+            pa = keep.tile([P, PACK, c1 - c0], F32, name=f"pa{c0}")
+            pb = keep.tile([P, PACK, c1 - c0], F32, name=f"pb{c0}")
+            for t in range(PACK):
+                nc.vector.tensor_tensor(pa[:, t, :], y_neg[t][:].indirect(entries(n1_sb, c0, c1)), y_pos[t][:, c0:c1], ALU.add)
+                nc.vector.tensor_tensor(pb[:, t, :], y_pos[t][:].indirect(entries(n2_sb, c0, c1)), y_neg[t][:, c0:c1], ALU.add)
+            rounded = []
+            for name, values in (("pa", pa), ("pb", pb)):
+                grouped = keep.tile([P, c1 - c0, PACK], BF16, name=f"{name}_bf{c0}", align_bytes=64)
+                nc.scalar.copy(
+                    grouped[:].rearrange("p (c i) t -> p c t i", i=4), values[:].rearrange("p t (c i) -> p c t i", i=4)
+                )
+                rounded.append(grouped[:].rearrange("p c t -> p (c t)"))
+            return rounded
+
+        h_banks = [psum.tile([P, S], F32, name=f"h_bank{t}") for t in range(PACK)]
+        h_sb = [keep.tile([P, S], F32, name=f"h_sb{t}") for t in range(PACK)]
+        h_less = [keep.tile([P, S], F32, name=f"h_less{t}") for t in range(PACK)]
+        d_word_picked = keep.tile([P, H], U32, name="d_word_picked")
+        d_word_dealt = keep.tile([P, PACK, P], U32, name="d_word_dealt", align_bytes=64)
+
+        def leave_bank(t, c0, c1):
+            nc.scalar.activation(h_sb[t][:, c0:c1], h_banks[t][:, c0:c1], COPY, scale=0.0625)
+            nc.scalar.activation(h_less[t][:, c0:c1], h_banks[t][:, c0:c1], COPY, scale=-0.75 * 0.0625)
+
+        def second_product(c0, c1, pa_bf, pb_bf):
+            width = PACK * (c1 - c0)
+            low = keep.tile([P, width], BF16, name=f"low{c0}")
+            high = keep.tile([P, width], BF16, name=f"high{c0}")
+            raised = keep.tile([P, width], BF16, name=f"raised{c0}")
+            z_bf = keep.tile([P, width], BF16, name=f"z_bf{c0}", align_bytes=64)
+            nc.vector.tensor_scalar_min(low[:], pb_bf, 0.0)
+            nc.vector.tensor_scalar_max(high[:], pb_bf, 0.0)
+            nc.vector.tensor_tensor(raised[:], pa_bf, low[:], ALU.max)
+            nc.vector.tensor_tensor(z_bf[:], raised[:], high[:], ALU.min)
+            z_words = keep.tile([P, c1 - c0], U32, name=f"z_words{c0}", align_bytes=64)
+            z_scales = keep.tile([P, c1 - c0], U8, name=f"z_scales{c0}", align_bytes=64)
+            nc.vector.quantize_mx(out=z_words[:].bitcast(FP8X4), scales=z_scales[:], in_=z_bf[:])
+            for t in range(PACK):
+                nc.tensor.matmul_mx(
+                    out=h_banks[t][:, c0:c1],
+                    lhsT=d_word_dealt[:, t, :].bitcast(FP8X4),
+                    lhsT_scale=d_scale_plane[:, t * P : (t + 1) * P],
+                    rhs=z_words[:].bitcast(FP8X4),
+                    rhs_scale=z_scales[:],
+                    start=True,
+                    stop=True,
+                )
+            leave_bank(0, c0, c1)
+
+        rounded = [differences(*CHUNKS[0]), differences(*CHUNKS[1])]
+        nc.vector.tensor_copy(d_word_picked[:], d_word_table[:].indirect(k1_sb[:]))
+        nc.vector.tensor_copy(
+            d_word_dealt[:].rearrange("p t m -> p m t"), d_word_picked[:].rearrange("p (m t) -> p m t", t=PACK)
+        )
+        second_product(*CHUNKS[0], *rounded[0])
+        rounded.append(differences(*CHUNKS[2]))
+        second_product(*CHUNKS[1], *rounded[1])
+        second_product(*CHUNKS[2], *rounded[2])
+
+        out_rows = out.rearrange("(p t) j -> p t j", t=PACK)
+        for t in range(PACK):
+            if t > 0:
+                leave_bank(t, 0, S)
+            for c0, c1 in HALVES:
+                third = keep.tile([P, c1 - c0], F32, name=f"third{t}_{c0}")
+                fourth = keep.tile([P, c1 - c0], F32, name=f"fourth{t}_{c0}")
+                result = keep.tile([P, c1 - c0], F32, name=f"result{t}_{c0}")
+                nc.vector.tensor_tensor(third[:], h_sb[t][:].indirect(entries(n3_sb, c0, c1)), h_less[t][:, c0:c1], ALU.add)
+                nc.vector.tensor_tensor(fourth[:], h_sb[t][:].indirect(entries(n4_sb, c0, c1)), h_less[t][:, c0:c1], ALU.add)
+                nc.vector.tensor_tensor(result[:], third[:], fourth[:], ALU.max)
+                nc.sync.dma_start(out_rows[:, t, c0:c1], result[:])

@@ -17,7 +17,9 @@ COPY = mybir.ActivationFunctionType.Copy
 
 P = 128
 PACK = 4
-CHUNKS = ((0, 256), (256, 384), (384, 512))
+QUARTER = 128
+QW = PACK * QUARTER
+LAST_PIECES = ((0, 256), (256, 384), (384, 512))
 HALVES = ((0, 256), (256, 512))
 
 
@@ -44,31 +46,31 @@ def tile_picked_denseminmodover_none_p_kernel(
         d_scale_plane = keep.tile([P, H], U8, name="d_scale_plane", align_bytes=64)
         x_word_table = keep.tile([P, T], U32, name="x_word_table")
         d_word_table = keep.tile([P, G], U32, name="d_word_table")
-        w_raw = [keep.tile([P, PACK, H // 2], F32, name=f"w_raw{u}") for u in range(2)]
+        w_raw = [keep.tile([P, PACK, H // 2], F32, name=f"w_raw{u}", tag=f"w_raw{u}") for u in range(2)]
         gs_sb = keep.tile([P, PACK], F32, name="gs_sb")
         gs_neg = keep.tile([P, PACK], F32, name="gs_neg")
 
-        nc.vector.memset(x_scale_table[:].bitcast(I32), 0)
-        nc.gpsimd.memset(d_scale_table[:].bitcast(I32), 0)
+        nc.gpsimd.memset(x_scale_table[:].bitcast(I32), 0)
+        nc.vector.memset(d_scale_table[:].bitcast(I32), 0)
 
         w_rows = w1.rearrange("(p j) c -> p j c", j=PACK)
+        nc.gpsimd.dma_start(gs_sb[:], gs.rearrange("(p t) o -> p (t o)", t=PACK))
         nc.sync.dma_start(offs_sb[:], offs)
         nc.sync.dma_start(x_word_table[:].bitcast(I32), x_words[0].rearrange("p n t -> p (n t)").bitcast(I32))
         for q in range(4):
-            nc.scalar.dma_start(
+            nc.sync.dma_start(
                 x_scale_table[32 * q : 32 * q + 4, :].bitcast(I32), x_scales[0, 4 * q : 4 * q + 4, :].bitcast(I32)
             )
         for u in range(2):
             nc.sync.dma_start(w_raw[u][:], w_rows[:, :, u * (H // 2) : (u + 1) * (H // 2)])
+        nc.sync.dma_start(n1_sb[:], n1)
+        nc.sync.dma_start(n2_sb[:], n2)
+        nc.sync.dma_start(k1_sb[:], k1)
         d_scale_rows = d_scales[0].rearrange("(q r) n -> r q n", r=4)
         for r in range(4):
             first = 16 * (r // 2) + r % 2
-            nc.gpsimd.dma_start(d_scale_table[first:P:32, :].bitcast(I32), d_scale_rows[r].bitcast(I32))
-        nc.gpsimd.memset(d_scale_plane[:].bitcast(I32), 0)
-        nc.sync.dma_start(gs_sb[:], gs.rearrange("(p t) o -> p (t o)", t=PACK))
-        nc.sync.dma_start(k1_sb[:], k1)
-        nc.sync.dma_start(n1_sb[:], n1)
-        nc.sync.dma_start(n2_sb[:], n2)
+            nc.sync.dma_start(d_scale_table[first:P:32, :].bitcast(I32), d_scale_rows[r].bitcast(I32))
+        nc.vector.memset(d_scale_plane[:].bitcast(I32), 0)
         nc.sync.dma_start(d_word_table[:].bitcast(I32), d_words[0].rearrange("p n t -> p (n t)").bitcast(I32))
         nc.sync.dma_start(n3_sb[:], n3)
         nc.sync.dma_start(n4_sb[:], n4)
@@ -77,8 +79,8 @@ def tile_picked_denseminmodover_none_p_kernel(
 
         x_scale_picked = keep.tile([P, S], U8, name="x_scale_picked", align_bytes=64)
         x_word_picked = keep.tile([P, S], U32, name="x_word_picked", align_bytes=64)
-        nc.vector.tensor_copy(x_scale_picked[:], x_scale_table[:].indirect(offs_sb[:]))
         nc.vector.tensor_copy(x_word_picked[:], x_word_table[:].indirect(offs_sb[:]))
+        nc.vector.tensor_copy(x_scale_picked[:], x_scale_table[:].indirect(offs_sb[:]))
 
         w_grouped = keep.tile([P, PACK, P, PACK], BF16, name="w_grouped", align_bytes=64)
         for u, copy in enumerate((nc.scalar.copy, nc.vector.tensor_copy)):
@@ -87,16 +89,16 @@ def tile_picked_denseminmodover_none_p_kernel(
                 w_raw[u][:].rearrange("p j (m t) -> p m j t", t=PACK),
             )
 
-        y_pos, y_neg = [], []
+        y_banks, y_sb, y_own = [], [], [[], []]
         for t in range(PACK):
             w_words = keep.tile([P, P], U32, name=f"w_words{t}", align_bytes=64)
             w_scales = keep.tile([P, P], U8, name=f"w_scales{t}", align_bytes=64)
             nc.vector.quantize_mx(
                 out=w_words[:].bitcast(FP8X4), scales=w_scales[:], in_=w_grouped[:, t].rearrange("p m j -> p (m j)")
             )
-            y_bank = psum.tile([P, S], F32, name=f"y_bank{t}")
+            y_banks.append(psum.tile([P, S], F32, name=f"y_bank{t}"))
             nc.tensor.matmul_mx(
-                out=y_bank[:],
+                out=y_banks[t][:],
                 lhsT=w_words[:].bitcast(FP8X4),
                 lhsT_scale=w_scales[:],
                 rhs=x_word_picked[:].bitcast(FP8X4),
@@ -104,93 +106,132 @@ def tile_picked_denseminmodover_none_p_kernel(
                 start=True,
                 stop=True,
             )
-            y_pos.append(keep.tile([P, S], F32, name=f"y_pos{t}"))
-            y_neg.append(keep.tile([P, S], F32, name=f"y_neg{t}"))
-            nc.scalar.activation(y_pos[t][:], y_bank[:], COPY, scale=gs_sb[:, t : t + 1])
-            nc.scalar.activation(y_neg[t][:], y_bank[:], COPY, scale=gs_neg[:, t : t + 1])
 
-        d_scale_picked = keep.tile([P, H], U8, name="d_scale_picked")
+        def own_columns(t, u):
+            c0, c1 = HALVES[u]
+            y_own[u].append(keep.tile([P, c1 - c0], F32, name=f"y_own{u}_{t}"))
+            nc.scalar.activation(y_own[u][t][:], y_banks[t][:, c0:c1], COPY, scale=gs_neg[:, t : t + 1])
+
+        for t in range(PACK):
+            y_sb.append(keep.tile([P, S], F32, name=f"y_sb{t}"))
+            nc.scalar.activation(y_sb[t][:], y_banks[t][:], COPY, scale=gs_neg[:, t : t + 1])
+            own_columns(t, 0)
+        for t in range(PACK):
+            own_columns(t, 1)
+
+        d_scale_picked = keep.tile([P, H], U8, name="d_scale_picked", tag="w_raw1")
         d_scale_dealt = keep.tile([P, PACK, P], U8, name="d_scale_dealt")
         nc.vector.tensor_copy(d_scale_picked[:], d_scale_table[:].indirect(k1_sb[:]))
-        nc.vector.tensor_copy(
-            d_scale_dealt[:].rearrange("p t m -> p m t"), d_scale_picked[:].rearrange("p (m t) -> p m t", t=PACK)
-        )
-        for r in range(4):
-            first = 16 * (r // 2) + r % 2
-            nc.sync.dma_start(
-                d_scale_plane[r:P:32, :].bitcast(I32),
-                d_scale_dealt[first:P:32].rearrange("p t m -> p (t m)").bitcast(I32),
+
+        pa = [keep.tile([P, PACK, S // 2], F32, name=f"pa{u}") for u in range(2)]
+        pb = [keep.tile([P, PACK, S // 2], F32, name=f"pb{u}") for u in range(2)]
+
+        def difference(values, places, t, u):
+            nc.vector.tensor_tensor(
+                values[u][:, t, :], y_sb[t][:].indirect(entries(places, *HALVES[u])), y_own[u][t][:], ALU.subtract
             )
 
-        def differences(c0, c1):
-            pa = keep.tile([P, PACK, c1 - c0], F32, name=f"pa{c0}")
-            pb = keep.tile([P, PACK, c1 - c0], F32, name=f"pb{c0}")
-            for t in range(PACK):
-                nc.vector.tensor_tensor(pa[:, t, :], y_neg[t][:].indirect(entries(n1_sb, c0, c1)), y_pos[t][:, c0:c1], ALU.add)
-                nc.vector.tensor_tensor(pb[:, t, :], y_pos[t][:].indirect(entries(n2_sb, c0, c1)), y_neg[t][:, c0:c1], ALU.add)
-            rounded = []
-            for name, values in (("pa", pa), ("pb", pb)):
-                grouped = keep.tile([P, c1 - c0, PACK], BF16, name=f"{name}_bf{c0}", align_bytes=64)
-                nc.scalar.copy(
-                    grouped[:].rearrange("p (c i) t -> p c t i", i=4), values[:].rearrange("p t (c i) -> p c t i", i=4)
+        def rounded(values, name, u, c0, c1, sign):
+            grouped = keep.tile([P, c1 - c0, PACK], BF16, name=f"{name}_bf{u}_{c0}")
+            nc.scalar.activation(
+                grouped[:].rearrange("p (c i) t -> p c t i", i=4),
+                values[u][:, :, c0:c1].rearrange("p t (c i) -> p c t i", i=4),
+                COPY,
+                scale=sign,
+            )
+            return grouped[:].rearrange("p c t -> p (c t)")
+
+        for t in range(PACK):
+            difference(pa, n1_sb, t, 0)
+            if t == 0:
+                nc.vector.tensor_copy(
+                    d_scale_dealt[:].rearrange("p t m -> p m t"),
+                    d_scale_picked[:].rearrange("p (m t) -> p m t", t=PACK),
                 )
-                rounded.append(grouped[:].rearrange("p c t -> p (c t)"))
-            return rounded
+                for r in range(4):
+                    first = 16 * (r // 2) + r % 2
+                    nc.sync.dma_start(
+                        d_scale_plane[r:P:32, :].bitcast(I32),
+                        d_scale_dealt[first:P:32].rearrange("p t m -> p (t m)").bitcast(I32),
+                    )
+            difference(pb, n2_sb, t, 0)
+
+        d_word_picked = keep.tile([P, H], U32, name="d_word_picked")
+        d_word_dealt = keep.tile([P, PACK, P], U32, name="d_word_dealt", align_bytes=64)
+        nc.vector.tensor_copy(d_word_picked[:], d_word_table[:].indirect(k1_sb[:]))
+        pa_bf = [rounded(pa, "pa", 0, 0, S // 2, 1.0)]
+        pb_bf = [rounded(pb, "pb", 0, 0, S // 2, -1.0)]
+        for t in range(PACK):
+            difference(pa, n1_sb, t, 1)
+            if t == 0:
+                nc.vector.tensor_copy(
+                    d_word_dealt[:].rearrange("p t m -> p m t"), d_word_picked[:].rearrange("p (m t) -> p m t", t=PACK)
+                )
+        pa_bf.append(rounded(pa, "pa", 1, 0, S // 2, 1.0))
+        for t in range(PACK):
+            difference(pb, n2_sb, t, 1)
+        pb_quarters = [pb_bf[0][:, :QW], pb_bf[0][:, QW:]]
+        pb_quarters.append(rounded(pb, "pb", 1, 0, QUARTER, -1.0))
+        pb_quarters.append(rounded(pb, "pb", 1, QUARTER, 2 * QUARTER, -1.0))
+        pa_quarters = [pa_bf[0][:, :QW], pa_bf[0][:, QW:], pa_bf[1][:, :QW], pa_bf[1][:, QW:]]
 
         h_banks = [psum.tile([P, S], F32, name=f"h_bank{t}") for t in range(PACK)]
         h_sb = [keep.tile([P, S], F32, name=f"h_sb{t}") for t in range(PACK)]
         h_less = [keep.tile([P, S], F32, name=f"h_less{t}") for t in range(PACK)]
-        d_word_picked = keep.tile([P, H], U32, name="d_word_picked")
-        d_word_dealt = keep.tile([P, PACK, P], U32, name="d_word_dealt", align_bytes=64)
 
         def leave_bank(t, c0, c1):
             nc.scalar.activation(h_sb[t][:, c0:c1], h_banks[t][:, c0:c1], COPY, scale=0.0625)
             nc.scalar.activation(h_less[t][:, c0:c1], h_banks[t][:, c0:c1], COPY, scale=-0.75 * 0.0625)
 
-        def second_product(c0, c1, pa_bf, pb_bf):
-            width = PACK * (c1 - c0)
-            low = keep.tile([P, width], BF16, name=f"low{c0}")
-            high = keep.tile([P, width], BF16, name=f"high{c0}")
-            raised = keep.tile([P, width], BF16, name=f"raised{c0}")
-            z_bf = keep.tile([P, width], BF16, name=f"z_bf{c0}", align_bytes=64)
-            nc.vector.tensor_scalar_min(low[:], pb_bf, 0.0)
-            nc.vector.tensor_scalar_max(high[:], pb_bf, 0.0)
-            nc.vector.tensor_tensor(raised[:], pa_bf, low[:], ALU.max)
-            nc.vector.tensor_tensor(z_bf[:], raised[:], high[:], ALU.min)
-            z_words = keep.tile([P, c1 - c0], U32, name=f"z_words{c0}", align_bytes=64)
-            z_scales = keep.tile([P, c1 - c0], U8, name=f"z_scales{c0}", align_bytes=64)
-            nc.vector.quantize_mx(out=z_words[:].bitcast(FP8X4), scales=z_scales[:], in_=z_bf[:])
-            for t in range(PACK):
-                nc.tensor.matmul_mx(
-                    out=h_banks[t][:, c0:c1],
-                    lhsT=d_word_dealt[:, t, :].bitcast(FP8X4),
-                    lhsT_scale=d_scale_plane[:, t * P : (t + 1) * P],
-                    rhs=z_words[:].bitcast(FP8X4),
-                    rhs_scale=z_scales[:],
-                    start=True,
-                    stop=True,
-                )
-            leave_bank(0, c0, c1)
-
-        rounded = [differences(*CHUNKS[0]), differences(*CHUNKS[1])]
-        nc.vector.tensor_copy(d_word_picked[:], d_word_table[:].indirect(k1_sb[:]))
-        nc.vector.tensor_copy(
-            d_word_dealt[:].rearrange("p t m -> p m t"), d_word_picked[:].rearrange("p (m t) -> p m t", t=PACK)
-        )
-        second_product(*CHUNKS[0], *rounded[0])
-        rounded.append(differences(*CHUNKS[2]))
-        second_product(*CHUNKS[1], *rounded[1])
-        second_product(*CHUNKS[2], *rounded[2])
+        for pair in ((0, 1), (2, 3)):
+            low = {v: keep.tile([P, QW], BF16, name=f"low{v}") for v in pair}
+            high = {v: keep.tile([P, QW], BF16, name=f"high{v}") for v in pair}
+            raised = {v: keep.tile([P, QW], BF16, name=f"raised{v}") for v in pair}
+            z_bf = {v: keep.tile([P, QW], BF16, name=f"z_bf{v}", align_bytes=64) for v in pair}
+            for v in pair:
+                nc.vector.tensor_scalar_min(low[v][:], pb_quarters[v], 0.0)
+                nc.vector.tensor_scalar_max(high[v][:], pb_quarters[v], 0.0)
+            for v in pair:
+                nc.vector.tensor_tensor(raised[v][:], pa_quarters[v], low[v][:], ALU.max)
+            for v in pair:
+                nc.vector.tensor_tensor(z_bf[v][:], raised[v][:], high[v][:], ALU.min)
+            for v in pair:
+                c0, c1 = v * QUARTER, (v + 1) * QUARTER
+                z_words = keep.tile([P, QUARTER], U32, name=f"z_words{v}", align_bytes=64)
+                z_scales = keep.tile([P, QUARTER], U8, name=f"z_scales{v}", align_bytes=64)
+                nc.vector.quantize_mx(out=z_words[:].bitcast(FP8X4), scales=z_scales[:], in_=z_bf[v][:])
+                for t in range(PACK):
+                    nc.tensor.matmul_mx(
+                        out=h_banks[t][:, c0:c1],
+                        lhsT=d_word_dealt[:, t, :].bitcast(FP8X4),
+                        lhsT_scale=d_scale_plane[:, t * P : (t + 1) * P],
+                        rhs=z_words[:].bitcast(FP8X4),
+                        rhs_scale=z_scales[:],
+                        start=True,
+                        stop=True,
+                    )
+                if v != 0:
+                    leave_bank(0, c0 if v > 1 else 0, c1)
 
         out_rows = out.rearrange("(p t) j -> p t j", t=PACK)
-        for t in range(PACK):
-            if t > 0:
-                leave_bank(t, 0, S)
-            for c0, c1 in HALVES:
-                third = keep.tile([P, c1 - c0], F32, name=f"third{t}_{c0}")
-                fourth = keep.tile([P, c1 - c0], F32, name=f"fourth{t}_{c0}")
-                result = keep.tile([P, c1 - c0], F32, name=f"result{t}_{c0}")
-                nc.vector.tensor_tensor(third[:], h_sb[t][:].indirect(entries(n3_sb, c0, c1)), h_less[t][:, c0:c1], ALU.add)
-                nc.vector.tensor_tensor(fourth[:], h_sb[t][:].indirect(entries(n4_sb, c0, c1)), h_less[t][:, c0:c1], ALU.add)
-                nc.vector.tensor_tensor(result[:], third[:], fourth[:], ALU.max)
-                nc.sync.dma_start(out_rows[:, t, c0:c1], result[:])
+        pieces = [(t, c0, c1) for t in range(PACK) for c0, c1 in (HALVES if t < PACK - 1 else LAST_PIECES)]
+
+        def fetch(places, name, t, c0, c1):
+            values = keep.tile([P, c1 - c0], F32, name=f"{name}{t}_{c0}")
+            nc.vector.tensor_tensor(values[:], h_sb[t][:].indirect(entries(places, c0, c1)), h_less[t][:, c0:c1], ALU.add)
+            return values
+
+        def finish(third, fourth, t, c0, c1):
+            result = keep.tile([P, c1 - c0], F32, name=f"result{t}_{c0}")
+            nc.vector.tensor_tensor(result[:], third[:], fourth[:], ALU.max)
+            nc.sync.dma_start(out_rows[:, t, c0:c1], result[:])
+
+        for t in range(1, PACK):
+            leave_bank(t, 0, S)
+        waiting = None
+        for piece in pieces:
+            third = fetch(n3_sb, "third", *piece)
+            if waiting is not None:
+                finish(*waiting)
+            waiting = (third, fetch(n4_sb, "fourth", *piece), *piece)
+        finish(*waiting)

@@ -14,9 +14,11 @@ U8 = mybir.dt.uint8
 FP8X4 = mybir.dt.float8_e4m3fn_x4
 ALU = mybir.AluOpType
 COPY = mybir.ActivationFunctionType.Copy
+RELU = mybir.ActivationFunctionType.Relu
 
 P = 128
 PACK = 4
+WHOLE = ((0, 512),)
 QUARTER = 128
 QW = PACK * QUARTER
 LAST_PIECES = ((0, 256), (256, 384), (384, 512))
@@ -46,80 +48,89 @@ def tile_picked_denseminmodover_none_p_kernel(
         d_scale_plane = keep.tile([P, H], U8, name="d_scale_plane", align_bytes=64)
         x_word_table = keep.tile([P, T], U32, name="x_word_table")
         d_word_table = keep.tile([P, G], U32, name="d_word_table")
-        w_raw = [keep.tile([P, PACK, H // 2], F32, name=f"w_raw{u}", tag=f"w_raw{u}") for u in range(2)]
+        w_raw = [keep.tile([P, PACK, H // 2], F32, name=f"w_raw{u}") for u in range(2)]
         gs_sb = keep.tile([P, PACK], F32, name="gs_sb")
-        gs_neg = keep.tile([P, PACK], F32, name="gs_neg")
 
-        nc.gpsimd.memset(x_scale_table[:].bitcast(I32), 0)
+        nc.vector.memset(x_scale_table[:].bitcast(I32), 0)
         nc.vector.memset(d_scale_table[:].bitcast(I32), 0)
 
-        w_rows = w1.rearrange("(p j) c -> p j c", j=PACK)
         nc.gpsimd.dma_start(gs_sb[:], gs.rearrange("(p t) o -> p (t o)", t=PACK))
+        w_rows = w1.rearrange("(p j) c -> p j c", j=PACK)
+        nc.sync.dma_start(w_raw[0][:], w_rows[:, :, : H // 2])
         nc.sync.dma_start(offs_sb[:], offs)
-        nc.sync.dma_start(x_word_table[:].bitcast(I32), x_words[0].rearrange("p n t -> p (n t)").bitcast(I32))
+        nc.sync.dma_start(w_raw[1][:], w_rows[:, :, H // 2 :])
         for q in range(4):
             nc.sync.dma_start(
                 x_scale_table[32 * q : 32 * q + 4, :].bitcast(I32), x_scales[0, 4 * q : 4 * q + 4, :].bitcast(I32)
             )
-        for u in range(2):
-            nc.sync.dma_start(w_raw[u][:], w_rows[:, :, u * (H // 2) : (u + 1) * (H // 2)])
-        nc.sync.dma_start(n1_sb[:], n1)
-        nc.sync.dma_start(n2_sb[:], n2)
+        nc.sync.dma_start(x_word_table[:].bitcast(I32), x_words[0].rearrange("p n t -> p (n t)").bitcast(I32))
         nc.sync.dma_start(k1_sb[:], k1)
         d_scale_rows = d_scales[0].rearrange("(q r) n -> r q n", r=4)
         for r in range(4):
             first = 16 * (r // 2) + r % 2
             nc.sync.dma_start(d_scale_table[first:P:32, :].bitcast(I32), d_scale_rows[r].bitcast(I32))
         nc.vector.memset(d_scale_plane[:].bitcast(I32), 0)
+        nc.sync.dma_start(n1_sb[:], n1)
+        nc.sync.dma_start(n2_sb[:], n2)
         nc.sync.dma_start(d_word_table[:].bitcast(I32), d_words[0].rearrange("p n t -> p (n t)").bitcast(I32))
         nc.sync.dma_start(n3_sb[:], n3)
         nc.sync.dma_start(n4_sb[:], n4)
 
-        nc.scalar.activation(gs_neg[:], gs_sb[:], COPY, scale=-1.0)
-
-        x_scale_picked = keep.tile([P, S], U8, name="x_scale_picked", align_bytes=64)
-        x_word_picked = keep.tile([P, S], U32, name="x_word_picked", align_bytes=64)
-        nc.vector.tensor_copy(x_word_picked[:], x_word_table[:].indirect(offs_sb[:]))
-        nc.vector.tensor_copy(x_scale_picked[:], x_scale_table[:].indirect(offs_sb[:]))
-
         w_grouped = keep.tile([P, PACK, P, PACK], BF16, name="w_grouped", align_bytes=64)
-        for u, copy in enumerate((nc.scalar.copy, nc.vector.tensor_copy)):
+        for u, copy in enumerate((nc.vector.tensor_copy, nc.scalar.copy)):
             copy(
                 w_grouped[:, :, u * (P // 2) : (u + 1) * (P // 2), :].rearrange("p t m j -> p m j t"),
                 w_raw[u][:].rearrange("p j (m t) -> p m j t", t=PACK),
             )
-
-        y_banks, y_sb, y_own = [], [], [[], []]
+        x_scale_picked = keep.tile([P, S], U8, name="x_scale_picked", align_bytes=64)
+        x_word_picked = keep.tile([P, S], U32, name="x_word_picked", align_bytes=64)
+        nc.vector.tensor_copy(x_scale_picked[:], x_scale_table[:].indirect(offs_sb[:]))
+        w_words = [keep.tile([P, P], U32, name=f"w_words{t}", align_bytes=64) for t in range(PACK)]
+        w_scales = [keep.tile([P, P], U8, name=f"w_scales{t}", align_bytes=64) for t in range(PACK)]
         for t in range(PACK):
-            w_words = keep.tile([P, P], U32, name=f"w_words{t}", align_bytes=64)
-            w_scales = keep.tile([P, P], U8, name=f"w_scales{t}", align_bytes=64)
             nc.vector.quantize_mx(
-                out=w_words[:].bitcast(FP8X4), scales=w_scales[:], in_=w_grouped[:, t].rearrange("p m j -> p (m j)")
+                out=w_words[t][:].bitcast(FP8X4), scales=w_scales[t][:], in_=w_grouped[:, t].rearrange("p m j -> p (m j)")
             )
-            y_banks.append(psum.tile([P, S], F32, name=f"y_bank{t}"))
+        for c0, c1 in HALVES:
+            nc.vector.tensor_copy(x_word_picked[:, c0:c1], x_word_table[:].indirect(entries(offs_sb, c0, c1)))
+
+        def first_product(t, c0, c1, tag):
+            bank = psum.tile([P, c1 - c0], F32, name=f"y_bank{t}_{c0}", tag=tag)
             nc.tensor.matmul_mx(
-                out=y_banks[t][:],
-                lhsT=w_words[:].bitcast(FP8X4),
-                lhsT_scale=w_scales[:],
-                rhs=x_word_picked[:].bitcast(FP8X4),
-                rhs_scale=x_scale_picked[:],
+                out=bank[:],
+                lhsT=w_words[t][:].bitcast(FP8X4),
+                lhsT_scale=w_scales[t][:],
+                rhs=x_word_picked[:, c0:c1].bitcast(FP8X4),
+                rhs_scale=x_scale_picked[:, c0:c1],
                 start=True,
                 stop=True,
             )
+            return bank
 
-        def own_columns(t, u):
-            c0, c1 = HALVES[u]
-            y_own[u].append(keep.tile([P, c1 - c0], F32, name=f"y_own{u}_{t}"))
-            nc.scalar.activation(y_own[u][t][:], y_banks[t][:, c0:c1], COPY, scale=gs_neg[:, t : t + 1])
+        y_halves = [[first_product(0, *HALVES[0], "bank7")[:], first_product(0, *HALVES[1], "bank0")[:]]]
+        y_banks = [None]
+        for t in range(1, PACK):
+            y_banks.append(first_product(t, 0, S, f"bank{t}"))
+            y_halves.append([y_banks[t][:, c0:c1] for c0, c1 in HALVES])
 
+        y_sb = [keep.tile([P, S], F32, name=f"y_sb{t}") for t in range(PACK)]
+        h_sb = [keep.tile([P, 2 * S if t in (1, 2) else S], F32, name=f"h_sb{t}") for t in range(PACK)]
+        own = [h_sb[t][:, S:] if t in (1, 2) else keep.tile([P, S], F32, name=f"y_own{t}")[:] for t in range(PACK)]
+        y_own = [[own[t][:, c0:c1] for t in range(PACK)] for c0, c1 in HALVES]
+
+        def weighted(target, source, t):
+            nc.scalar.activation(target, source, COPY, scale=gs_sb[:, t : t + 1])
+
+        weighted(y_sb[0][:, : S // 2], y_halves[0][0], 0)
+        weighted(y_own[0][0], y_halves[0][0], 0)
+        weighted(y_sb[0][:, S // 2 :], y_halves[0][1], 0)
+        for t in range(1, PACK):
+            weighted(y_sb[t][:], y_banks[t][:], t)
+            weighted(y_own[0][t], y_halves[t][0], t)
         for t in range(PACK):
-            y_sb.append(keep.tile([P, S], F32, name=f"y_sb{t}"))
-            nc.scalar.activation(y_sb[t][:], y_banks[t][:], COPY, scale=gs_neg[:, t : t + 1])
-            own_columns(t, 0)
-        for t in range(PACK):
-            own_columns(t, 1)
+            weighted(y_own[1][t], y_halves[t][1], t)
 
-        d_scale_picked = keep.tile([P, H], U8, name="d_scale_picked", tag="w_raw1")
+        d_scale_picked = keep.tile([P, H], U8, name="d_scale_picked")
         d_scale_dealt = keep.tile([P, PACK, P], U8, name="d_scale_dealt")
         nc.vector.tensor_copy(d_scale_picked[:], d_scale_table[:].indirect(k1_sb[:]))
 
@@ -128,15 +139,15 @@ def tile_picked_denseminmodover_none_p_kernel(
 
         def difference(values, places, t, u):
             nc.vector.tensor_tensor(
-                values[u][:, t, :], y_sb[t][:].indirect(entries(places, *HALVES[u])), y_own[u][t][:], ALU.subtract
+                values[u][:, t, :], y_sb[t][:].indirect(entries(places, *HALVES[u])), y_own[u][t], ALU.subtract
             )
 
-        def rounded(values, name, u, c0, c1, sign):
+        def rounded(values, name, u, c0, c1, func, sign):
             grouped = keep.tile([P, c1 - c0, PACK], BF16, name=f"{name}_bf{u}_{c0}")
             nc.scalar.activation(
                 grouped[:].rearrange("p (c i) t -> p c t i", i=4),
                 values[u][:, :, c0:c1].rearrange("p t (c i) -> p c t i", i=4),
-                COPY,
+                func,
                 scale=sign,
             )
             return grouped[:].rearrange("p c t -> p (c t)")
@@ -145,8 +156,8 @@ def tile_picked_denseminmodover_none_p_kernel(
             difference(pa, n1_sb, t, 0)
             if t == 0:
                 nc.vector.tensor_copy(
-                    d_scale_dealt[:].rearrange("p t m -> p m t"),
-                    d_scale_picked[:].rearrange("p (m t) -> p m t", t=PACK),
+                    d_scale_dealt[:].bitcast(I32).rearrange("p t (g w) -> p t g w", g=8),
+                    d_scale_picked[:].bitcast(I32).rearrange("p (g t w) -> p t g w", g=8, t=PACK),
                 )
                 for r in range(4):
                     first = 16 * (r // 2) + r % 2
@@ -159,42 +170,49 @@ def tile_picked_denseminmodover_none_p_kernel(
         d_word_picked = keep.tile([P, H], U32, name="d_word_picked")
         d_word_dealt = keep.tile([P, PACK, P], U32, name="d_word_dealt", align_bytes=64)
         nc.vector.tensor_copy(d_word_picked[:], d_word_table[:].indirect(k1_sb[:]))
-        pa_bf = [rounded(pa, "pa", 0, 0, S // 2, 1.0)]
-        pb_bf = [rounded(pb, "pb", 0, 0, S // 2, -1.0)]
         for t in range(PACK):
-            difference(pa, n1_sb, t, 1)
-            if t == 0:
-                nc.vector.tensor_copy(
-                    d_word_dealt[:].rearrange("p t m -> p m t"), d_word_picked[:].rearrange("p (m t) -> p m t", t=PACK)
-                )
-        pa_bf.append(rounded(pa, "pa", 1, 0, S // 2, 1.0))
+            nc.sync.dma_start(
+                d_word_dealt[:, t, :].bitcast(I32).rearrange("p (g r) -> p g r", g=8),
+                d_word_picked[:].bitcast(I32).rearrange("p (g t r) -> p t g r", g=8, t=PACK)[:, t],
+            )
+        pa_bf = [rounded(pa, "pa", 0, 0, S // 2, COPY, -1.0)]
+        pb_bf = [rounded(pb, "pb", 0, 0, S // 2, COPY, 1.0)]
+        high_bf = [rounded(pb, "high", 0, 0, S // 2, RELU, 1.0)]
         for t in range(PACK):
             difference(pb, n2_sb, t, 1)
-        pb_quarters = [pb_bf[0][:, :QW], pb_bf[0][:, QW:]]
-        pb_quarters.append(rounded(pb, "pb", 1, 0, QUARTER, -1.0))
-        pb_quarters.append(rounded(pb, "pb", 1, QUARTER, 2 * QUARTER, -1.0))
-        pa_quarters = [pa_bf[0][:, :QW], pa_bf[0][:, QW:], pa_bf[1][:, :QW], pa_bf[1][:, QW:]]
+        pb_bf.append(rounded(pb, "pb", 1, 0, S // 2, COPY, 1.0))
+        high_bf.append(rounded(pb, "high", 1, 0, S // 2, RELU, 1.0))
+        for t in range(PACK):
+            difference(pa, n1_sb, t, 1)
+        pa_bf.append(rounded(pa, "pa", 1, 0, S // 2, COPY, -1.0))
 
-        h_banks = [psum.tile([P, S], F32, name=f"h_bank{t}") for t in range(PACK)]
-        h_sb = [keep.tile([P, S], F32, name=f"h_sb{t}") for t in range(PACK)]
+        def quarter(halves, v):
+            return halves[v // 2][:, (v % 2) * QW : (v % 2 + 1) * QW]
+
+        h_banks = [psum.tile([P, S], F32, name=f"h_bank{t}", tag=f"bank{4 + t}") for t in range(PACK)]
         h_less = [keep.tile([P, S], F32, name=f"h_less{t}") for t in range(PACK)]
 
-        def leave_bank(t, c0, c1):
-            nc.scalar.activation(h_sb[t][:, c0:c1], h_banks[t][:, c0:c1], COPY, scale=0.0625)
-            nc.scalar.activation(h_less[t][:, c0:c1], h_banks[t][:, c0:c1], COPY, scale=-0.75 * 0.0625)
+        late_banks = {v: psum.tile([P, QUARTER], F32, name=f"late_bank{v}", tag=f"bank{v - 2}") for v in (2, 3)}
 
-        for pair in ((0, 1), (2, 3)):
+        def h_sums(t, c0, c1):
+            v = c0 // QUARTER
+            return late_banks[v][:] if t == 0 and v in late_banks else h_banks[t][:, c0:c1]
+
+        def leave_bank(t, c0, c1):
+            nc.scalar.activation(h_sb[t][:, c0:c1], h_sums(t, c0, c1), COPY, scale=0.0625)
+            nc.scalar.activation(h_less[t][:, c0:c1], h_sums(t, c0, c1), COPY, scale=-0.75 * 0.0625)
+
+        for u in range(2):
+            pair = (2 * u, 2 * u + 1)
             low = {v: keep.tile([P, QW], BF16, name=f"low{v}") for v in pair}
-            high = {v: keep.tile([P, QW], BF16, name=f"high{v}") for v in pair}
             raised = {v: keep.tile([P, QW], BF16, name=f"raised{v}") for v in pair}
             z_bf = {v: keep.tile([P, QW], BF16, name=f"z_bf{v}", align_bytes=64) for v in pair}
             for v in pair:
-                nc.vector.tensor_scalar_min(low[v][:], pb_quarters[v], 0.0)
-                nc.vector.tensor_scalar_max(high[v][:], pb_quarters[v], 0.0)
+                nc.vector.tensor_scalar_min(low[v][:], quarter(pb_bf, v), 0.0)
             for v in pair:
-                nc.vector.tensor_tensor(raised[v][:], pa_quarters[v], low[v][:], ALU.max)
+                nc.vector.tensor_tensor(raised[v][:], quarter(pa_bf, v), low[v][:], ALU.max)
             for v in pair:
-                nc.vector.tensor_tensor(z_bf[v][:], raised[v][:], high[v][:], ALU.min)
+                nc.vector.tensor_tensor(z_bf[v][:], raised[v][:], quarter(high_bf, v), ALU.min)
             for v in pair:
                 c0, c1 = v * QUARTER, (v + 1) * QUARTER
                 z_words = keep.tile([P, QUARTER], U32, name=f"z_words{v}", align_bytes=64)
@@ -202,7 +220,7 @@ def tile_picked_denseminmodover_none_p_kernel(
                 nc.vector.quantize_mx(out=z_words[:].bitcast(FP8X4), scales=z_scales[:], in_=z_bf[v][:])
                 for t in range(PACK):
                     nc.tensor.matmul_mx(
-                        out=h_banks[t][:, c0:c1],
+                        out=h_sums(t, c0, c1),
                         lhsT=d_word_dealt[:, t, :].bitcast(FP8X4),
                         lhsT_scale=d_scale_plane[:, t * P : (t + 1) * P],
                         rhs=z_words[:].bitcast(FP8X4),
@@ -213,8 +231,8 @@ def tile_picked_denseminmodover_none_p_kernel(
                 if v != 0:
                     leave_bank(0, c0 if v > 1 else 0, c1)
 
-        out_rows = out.rearrange("(p t) j -> p t j", t=PACK)
-        pieces = [(t, c0, c1) for t in range(PACK) for c0, c1 in (HALVES if t < PACK - 1 else LAST_PIECES)]
+        out_rows = out.rearrange("(g t r) j -> t g r j", g=8, t=PACK)
+        pieces = [(t, c0, c1) for t in range(PACK) for c0, c1 in (HALVES, WHOLE, WHOLE, LAST_PIECES)[t]]
 
         def fetch(places, name, t, c0, c1):
             values = keep.tile([P, c1 - c0], F32, name=f"{name}{t}_{c0}")
@@ -224,7 +242,7 @@ def tile_picked_denseminmodover_none_p_kernel(
         def finish(third, fourth, t, c0, c1):
             result = keep.tile([P, c1 - c0], F32, name=f"result{t}_{c0}")
             nc.vector.tensor_tensor(result[:], third[:], fourth[:], ALU.max)
-            nc.sync.dma_start(out_rows[:, t, c0:c1], result[:])
+            nc.sync.dma_start(out_rows[t, :, :, c0:c1], result[:])
 
         for t in range(1, PACK):
             leave_bank(t, 0, S)

@@ -1,6 +1,7 @@
 from contextlib import ExitStack
 
 import concourse.mybir as mybir
+from concourse.masks import make_identity
 
 K, T, S, H, G = 512, 2048, 512, 512, 2048
 FLOPS = 2 * 2 * K * H * S
@@ -18,7 +19,6 @@ RELU = mybir.ActivationFunctionType.Relu
 
 P = 128
 PACK = 4
-WHOLE = ((0, 512),)
 QUARTER = 128
 QW = PACK * QUARTER
 LAST_PIECES = ((0, 256), (256, 384), (384, 512))
@@ -114,9 +114,7 @@ def tile_picked_denseminmodover_none_p_kernel(
             y_halves.append([y_banks[t][:, c0:c1] for c0, c1 in HALVES])
 
         y_sb = [keep.tile([P, S], F32, name=f"y_sb{t}") for t in range(PACK)]
-        h_sb = [keep.tile([P, 2 * S if t in (1, 2) else S], F32, name=f"h_sb{t}") for t in range(PACK)]
-        own = [h_sb[t][:, S:] if t in (1, 2) else keep.tile([P, S], F32, name=f"y_own{t}")[:] for t in range(PACK)]
-        y_own = [[own[t][:, c0:c1] for t in range(PACK)] for c0, c1 in HALVES]
+        y_own = [[keep.tile([P, S // 2], F32, name=f"y_own{u}_{t}")[:] for t in range(PACK)] for u in range(2)]
 
         def weighted(target, source, t):
             nc.scalar.activation(target, source, COPY, scale=gs_sb[:, t : t + 1])
@@ -190,6 +188,7 @@ def tile_picked_denseminmodover_none_p_kernel(
             return halves[v // 2][:, (v % 2) * QW : (v % 2 + 1) * QW]
 
         h_banks = [psum.tile([P, S], F32, name=f"h_bank{t}", tag=f"bank{4 + t}") for t in range(PACK)]
+        h_sb = [keep.tile([P, S], F32, name=f"h_sb{t}") for t in range(PACK)]
         h_less = [keep.tile([P, S], F32, name=f"h_less{t}") for t in range(PACK)]
 
         late_banks = {v: psum.tile([P, QUARTER], F32, name=f"late_bank{v}", tag=f"bank{v - 2}") for v in (2, 3)}
@@ -198,8 +197,10 @@ def tile_picked_denseminmodover_none_p_kernel(
             v = c0 // QUARTER
             return late_banks[v][:] if t == 0 and v in late_banks else h_banks[t][:, c0:c1]
 
-        def leave_bank(t, c0, c1):
+        def take_h(t, c0, c1):
             nc.scalar.activation(h_sb[t][:, c0:c1], h_sums(t, c0, c1), COPY, scale=0.0625)
+
+        def take_less(t, c0, c1):
             nc.scalar.activation(h_less[t][:, c0:c1], h_sums(t, c0, c1), COPY, scale=-0.75 * 0.0625)
 
         for u in range(2):
@@ -229,10 +230,11 @@ def tile_picked_denseminmodover_none_p_kernel(
                         stop=True,
                     )
                 if v != 0:
-                    leave_bank(0, c0 if v > 1 else 0, c1)
+                    take_h(0, c0 if v > 1 else 0, c1)
 
         out_rows = out.rearrange("(g t r) j -> t g r j", g=8, t=PACK)
-        pieces = [(t, c0, c1) for t in range(PACK) for c0, c1 in (HALVES, WHOLE, WHOLE, LAST_PIECES)[t]]
+        identity = keep.tile([P, P], F32, name="identity")
+        make_identity(nc, identity[:])
 
         def fetch(places, name, t, c0, c1):
             values = keep.tile([P, c1 - c0], F32, name=f"{name}{t}_{c0}")
@@ -244,8 +246,50 @@ def tile_picked_denseminmodover_none_p_kernel(
             nc.vector.tensor_tensor(result[:], third[:], fourth[:], ALU.max)
             nc.sync.dma_start(out_rows[t, :, :, c0:c1], result[:])
 
-        for t in range(1, PACK):
-            leave_bank(t, 0, S)
+        def finish_by_sums(third, rise, t, u):
+            c0, c1 = HALVES[u]
+            blocks = [slice(b * P, (b + 1) * P) for b in range((c1 - c0) // P)]
+            gain = keep.tile([P, c1 - c0], F32, name=f"gain{t}_{u}")
+            nc.scalar.activation(gain[:], rise[:], RELU)
+            sum_bank = psum.tile([P, c1 - c0], F32, name=f"sum_bank{t}_{u}", tag=f"bank{2 + u}")
+            terms = (third[:], h_less[t][:, c0:c1], gain[:])
+            for block in blocks:
+                for place, term in enumerate(terms):
+                    nc.tensor.matmul(
+                        sum_bank[:, block],
+                        lhsT=term[:, block],
+                        rhs=identity[:],
+                        is_transpose=True,
+                        start=place == 0,
+                        stop=place == len(terms) - 1,
+                    )
+            turned = keep.tile([P, c1 - c0], F32, name=f"turned{t}_{u}")
+            nc.scalar.copy(turned[:], sum_bank[:])
+            back_bank = psum.tile([P, c1 - c0], F32, name=f"back_bank{t}_{u}", tag=f"bank{u}")
+            for block in blocks:
+                nc.tensor.transpose(back_bank[:, block], turned[:, block], identity[:])
+            result = keep.tile([P, c1 - c0], F32, name=f"result{t}_{c0}")
+            nc.scalar.copy(result[:], back_bank[:])
+            nc.scalar.dma_start(out_rows[t, :, :, c0:c1], result[:])
+
+        take_h(1, 0, S)
+        for t in (2, 3):
+            take_h(t, 0, S)
+            take_less(t, 0, S)
+        nc.scalar.activation(h_less[0][:], h_sb[0][:], COPY, scale=-0.75)
+        take_less(1, 0, S)
+        for t in (0, 1):
+            thirds = [keep.tile([P, S // 2], F32, name=f"third{t}_{u}") for u in range(2)]
+            rises = [keep.tile([P, S // 2], F32, name=f"rise{t}_{u}") for u in range(2)]
+            for u in range(2):
+                nc.vector.tensor_copy(thirds[u][:], h_sb[t][:].indirect(entries(n3_sb, *HALVES[u])))
+            for u in range(2):
+                nc.vector.tensor_tensor(
+                    rises[u][:], h_sb[t][:].indirect(entries(n4_sb, *HALVES[u])), thirds[u][:], ALU.subtract
+                )
+                finish_by_sums(thirds[u], rises[u], t, u)
+
+        pieces = [(2, c0, c1) for c0, c1 in HALVES] + [(3, c0, c1) for c0, c1 in LAST_PIECES]
         waiting = None
         for piece in pieces:
             third = fetch(n3_sb, "third", *piece)

@@ -19,10 +19,15 @@ RELU = mybir.ActivationFunctionType.Relu
 
 P = 128
 PACK = 4
-QUARTER = 128
-QW = PACK * QUARTER
-LAST_PIECES = ((0, 256), (256, 384), (384, 512))
-HALVES = ((0, 256), (256, 512))
+RUNS = 8
+QUADRANT = 32
+LIST_ROWS = 16
+HALVES = ((0, S // 2), (S // 2, S))
+QUARTER = S // 4
+WIDE_TILES = (1, 2)
+LAST_PIECES = ((0, S // 2), (S // 2, 3 * S // 4), (3 * S // 4, S))
+H_FACTOR = 0.0625
+OWN_FACTOR = -0.75
 
 
 def tile_picked_denseminmodover_none_p_kernel(
@@ -35,17 +40,20 @@ def tile_picked_denseminmodover_none_p_kernel(
         psum = ctx.enter_context(tc.psum_pool(name="psum", bufs=1))
 
         def list_tile(name):
-            return lists.tile([P, S // 16], U16, name=name)
+            return lists.tile([P, S // LIST_ROWS], U16, name=name)
 
         def entries(tile, c0, c1):
-            return tile[:, c0 // 16 : c1 // 16]
+            return tile[:, c0 // LIST_ROWS : c1 // LIST_ROWS]
+
+        def gathered_scale_rows(tile, row):
+            return tile[LIST_ROWS * (row // 2) + row % 2 : P : QUADRANT]
 
         offs_sb, n1_sb, n2_sb = list_tile("offs_sb"), list_tile("n1_sb"), list_tile("n2_sb")
         k1_sb, n3_sb, n4_sb = list_tile("k1_sb"), list_tile("n3_sb"), list_tile("n4_sb")
 
         x_scale_table = keep.tile([P, T], U8, name="x_scale_table")
         d_scale_table = keep.tile([P, G], U8, name="d_scale_table")
-        d_scale_plane = keep.tile([P, H], U8, name="d_scale_plane", align_bytes=64)
+        d_scale_rows = keep.tile([P, H], U8, name="d_scale_rows", align_bytes=64)
         x_word_table = keep.tile([P, T], U32, name="x_word_table")
         d_word_table = keep.tile([P, G], U32, name="d_word_table")
         w_raw = [keep.tile([P, PACK, H // 2], F32, name=f"w_raw{u}") for u in range(2)]
@@ -59,17 +67,17 @@ def tile_picked_denseminmodover_none_p_kernel(
         nc.sync.dma_start(w_raw[0][:], w_rows[:, :, : H // 2])
         nc.sync.dma_start(offs_sb[:], offs)
         nc.sync.dma_start(w_raw[1][:], w_rows[:, :, H // 2 :])
-        for q in range(4):
+        for q in range(P // QUADRANT):
             nc.sync.dma_start(
-                x_scale_table[32 * q : 32 * q + 4, :].bitcast(I32), x_scales[0, 4 * q : 4 * q + 4, :].bitcast(I32)
+                x_scale_table[QUADRANT * q : QUADRANT * q + 4, :].bitcast(I32),
+                x_scales[0, 4 * q : 4 * q + 4, :].bitcast(I32),
             )
         nc.sync.dma_start(x_word_table[:].bitcast(I32), x_words[0].rearrange("p n t -> p (n t)").bitcast(I32))
         nc.sync.dma_start(k1_sb[:], k1)
-        d_scale_rows = d_scales[0].rearrange("(q r) n -> r q n", r=4)
-        for r in range(4):
-            first = 16 * (r // 2) + r % 2
-            nc.sync.dma_start(d_scale_table[first:P:32, :].bitcast(I32), d_scale_rows[r].bitcast(I32))
-        nc.vector.memset(d_scale_plane[:].bitcast(I32), 0)
+        d_scales_by_row = d_scales[0].rearrange("(q row) n -> row q n", row=4)
+        for row in range(4):
+            nc.sync.dma_start(gathered_scale_rows(d_scale_table, row).bitcast(I32), d_scales_by_row[row].bitcast(I32))
+        nc.vector.memset(d_scale_rows[:].bitcast(I32), 0)
         nc.sync.dma_start(n1_sb[:], n1)
         nc.sync.dma_start(n2_sb[:], n2)
         nc.sync.dma_start(d_word_table[:].bitcast(I32), d_words[0].rearrange("p n t -> p (n t)").bitcast(I32))
@@ -108,13 +116,15 @@ def tile_picked_denseminmodover_none_p_kernel(
             return bank
 
         y_halves = [[first_product(0, *HALVES[0], "bank7")[:], first_product(0, *HALVES[1], "bank0")[:]]]
-        y_banks = [None]
+        y_banks = {}
         for t in range(1, PACK):
-            y_banks.append(first_product(t, 0, S, f"bank{t}"))
+            y_banks[t] = first_product(t, 0, S, f"bank{t}")
             y_halves.append([y_banks[t][:, c0:c1] for c0, c1 in HALVES])
 
         y_sb = [keep.tile([P, S], F32, name=f"y_sb{t}") for t in range(PACK)]
-        y_own = [[keep.tile([P, S // 2], F32, name=f"y_own{u}_{t}")[:] for t in range(PACK)] for u in range(2)]
+        h_sb = [keep.tile([P, 2 * S if t in WIDE_TILES else S], F32, name=f"h_sb{t}") for t in range(PACK)]
+        own = [h_sb[t][:, S:] if t in WIDE_TILES else keep.tile([P, S], F32, name=f"y_own{t}")[:] for t in range(PACK)]
+        y_own = [[own[t][:, c0:c1] for t in range(PACK)] for c0, c1 in HALVES]
 
         def weighted(target, source, t):
             nc.scalar.activation(target, source, COPY, scale=gs_sb[:, t : t + 1])
@@ -132,7 +142,18 @@ def tile_picked_denseminmodover_none_p_kernel(
         d_scale_dealt = keep.tile([P, PACK, P], U8, name="d_scale_dealt")
         nc.vector.tensor_copy(d_scale_picked[:], d_scale_table[:].indirect(k1_sb[:]))
 
-        pa = [keep.tile([P, PACK, S // 2], F32, name=f"pa{u}") for u in range(2)]
+        def place_d_scales():
+            nc.vector.tensor_copy(
+                d_scale_dealt[:].bitcast(I32).rearrange("p t (g w) -> p t g w", g=RUNS),
+                d_scale_picked[:].bitcast(I32).rearrange("p (g t w) -> p t g w", g=RUNS, t=PACK),
+            )
+            for row in range(4):
+                nc.sync.dma_start(
+                    d_scale_rows[row:P:QUADRANT, :].bitcast(I32),
+                    gathered_scale_rows(d_scale_dealt, row).rearrange("p t m -> p (t m)").bitcast(I32),
+                )
+
+        pa_neg = [keep.tile([P, PACK, S // 2], F32, name=f"pa_neg{u}") for u in range(2)]
         pb = [keep.tile([P, PACK, S // 2], F32, name=f"pb{u}") for u in range(2)]
 
         def difference(values, places, t, u):
@@ -140,29 +161,21 @@ def tile_picked_denseminmodover_none_p_kernel(
                 values[u][:, t, :], y_sb[t][:].indirect(entries(places, *HALVES[u])), y_own[u][t], ALU.subtract
             )
 
-        def rounded(values, name, u, c0, c1, func, sign):
-            grouped = keep.tile([P, c1 - c0, PACK], BF16, name=f"{name}_bf{u}_{c0}")
+        def rounded(values, name, u, func, sign):
+            grouped = keep.tile([P, S // 2, PACK], BF16, name=f"{name}_bf{u}")
             nc.scalar.activation(
                 grouped[:].rearrange("p (c i) t -> p c t i", i=4),
-                values[u][:, :, c0:c1].rearrange("p t (c i) -> p c t i", i=4),
+                values[u][:].rearrange("p t (c i) -> p c t i", i=4),
                 func,
                 scale=sign,
             )
             return grouped[:].rearrange("p c t -> p (c t)")
 
-        for t in range(PACK):
-            difference(pa, n1_sb, t, 0)
-            if t == 0:
-                nc.vector.tensor_copy(
-                    d_scale_dealt[:].bitcast(I32).rearrange("p t (g w) -> p t g w", g=8),
-                    d_scale_picked[:].bitcast(I32).rearrange("p (g t w) -> p t g w", g=8, t=PACK),
-                )
-                for r in range(4):
-                    first = 16 * (r // 2) + r % 2
-                    nc.sync.dma_start(
-                        d_scale_plane[r:P:32, :].bitcast(I32),
-                        d_scale_dealt[first:P:32].rearrange("p t m -> p (t m)").bitcast(I32),
-                    )
+        difference(pa_neg, n1_sb, 0, 0)
+        place_d_scales()
+        difference(pb, n2_sb, 0, 0)
+        for t in range(1, PACK):
+            difference(pa_neg, n1_sb, t, 0)
             difference(pb, n2_sb, t, 0)
 
         d_word_picked = keep.tile([P, H], U32, name="d_word_picked")
@@ -170,27 +183,26 @@ def tile_picked_denseminmodover_none_p_kernel(
         nc.vector.tensor_copy(d_word_picked[:], d_word_table[:].indirect(k1_sb[:]))
         for t in range(PACK):
             nc.sync.dma_start(
-                d_word_dealt[:, t, :].bitcast(I32).rearrange("p (g r) -> p g r", g=8),
-                d_word_picked[:].bitcast(I32).rearrange("p (g t r) -> p t g r", g=8, t=PACK)[:, t],
+                d_word_dealt[:, t, :].bitcast(I32).rearrange("p (g r) -> p g r", g=RUNS),
+                d_word_picked[:].bitcast(I32).rearrange("p (g t r) -> p t g r", g=RUNS, t=PACK)[:, t],
             )
-        pa_bf = [rounded(pa, "pa", 0, 0, S // 2, COPY, -1.0)]
-        pb_bf = [rounded(pb, "pb", 0, 0, S // 2, COPY, 1.0)]
-        high_bf = [rounded(pb, "high", 0, 0, S // 2, RELU, 1.0)]
+
+        pa_bf = [rounded(pa_neg, "pa", 0, COPY, -1.0)]
+        pb_bf = [rounded(pb, "pb", 0, COPY, 1.0)]
+        high_bf = [rounded(pb, "high", 0, RELU, 1.0)]
         for t in range(PACK):
             difference(pb, n2_sb, t, 1)
-        pb_bf.append(rounded(pb, "pb", 1, 0, S // 2, COPY, 1.0))
-        high_bf.append(rounded(pb, "high", 1, 0, S // 2, RELU, 1.0))
+        pb_bf.append(rounded(pb, "pb", 1, COPY, 1.0))
+        high_bf.append(rounded(pb, "high", 1, RELU, 1.0))
         for t in range(PACK):
-            difference(pa, n1_sb, t, 1)
-        pa_bf.append(rounded(pa, "pa", 1, 0, S // 2, COPY, -1.0))
+            difference(pa_neg, n1_sb, t, 1)
+        pa_bf.append(rounded(pa_neg, "pa", 1, COPY, -1.0))
 
         def quarter(halves, v):
-            return halves[v // 2][:, (v % 2) * QW : (v % 2 + 1) * QW]
+            return halves[v // 2][:, (v % 2) * PACK * QUARTER : (v % 2 + 1) * PACK * QUARTER]
 
-        h_banks = [psum.tile([P, S], F32, name=f"h_bank{t}", tag=f"bank{4 + t}") for t in range(PACK)]
-        h_sb = [keep.tile([P, S], F32, name=f"h_sb{t}") for t in range(PACK)]
+        h_banks = [psum.tile([P, S], F32, name=f"h_bank{t}", tag=f"bank{PACK + t}") for t in range(PACK)]
         h_less = [keep.tile([P, S], F32, name=f"h_less{t}") for t in range(PACK)]
-
         late_banks = {v: psum.tile([P, QUARTER], F32, name=f"late_bank{v}", tag=f"bank{v - 2}") for v in (2, 3)}
 
         def h_sums(t, c0, c1):
@@ -198,16 +210,13 @@ def tile_picked_denseminmodover_none_p_kernel(
             return late_banks[v][:] if t == 0 and v in late_banks else h_banks[t][:, c0:c1]
 
         def take_h(t, c0, c1):
-            nc.scalar.activation(h_sb[t][:, c0:c1], h_sums(t, c0, c1), COPY, scale=0.0625)
-
-        def take_less(t, c0, c1):
-            nc.scalar.activation(h_less[t][:, c0:c1], h_sums(t, c0, c1), COPY, scale=-0.75 * 0.0625)
+            nc.scalar.activation(h_sb[t][:, c0:c1], h_sums(t, c0, c1), COPY, scale=H_FACTOR)
 
         for u in range(2):
             pair = (2 * u, 2 * u + 1)
-            low = {v: keep.tile([P, QW], BF16, name=f"low{v}") for v in pair}
-            raised = {v: keep.tile([P, QW], BF16, name=f"raised{v}") for v in pair}
-            z_bf = {v: keep.tile([P, QW], BF16, name=f"z_bf{v}", align_bytes=64) for v in pair}
+            low = {v: keep.tile([P, PACK * QUARTER], BF16, name=f"low{v}") for v in pair}
+            raised = {v: keep.tile([P, PACK * QUARTER], BF16, name=f"raised{v}") for v in pair}
+            z_bf = {v: keep.tile([P, PACK * QUARTER], BF16, name=f"z_bf{v}", align_bytes=64) for v in pair}
             for v in pair:
                 nc.vector.tensor_scalar_min(low[v][:], quarter(pb_bf, v), 0.0)
             for v in pair:
@@ -223,36 +232,33 @@ def tile_picked_denseminmodover_none_p_kernel(
                     nc.tensor.matmul_mx(
                         out=h_sums(t, c0, c1),
                         lhsT=d_word_dealt[:, t, :].bitcast(FP8X4),
-                        lhsT_scale=d_scale_plane[:, t * P : (t + 1) * P],
+                        lhsT_scale=d_scale_rows[:, t * P : (t + 1) * P],
                         rhs=z_words[:].bitcast(FP8X4),
                         rhs_scale=z_scales[:],
                         start=True,
                         stop=True,
                     )
-                if v != 0:
-                    take_h(0, c0 if v > 1 else 0, c1)
+                if v in late_banks:
+                    take_h(0, c0, c1)
+                elif c1 == S // 2:
+                    take_h(0, *HALVES[0])
 
-        out_rows = out.rearrange("(g t r) j -> t g r j", g=8, t=PACK)
+        out_rows = out.rearrange("(g t r) j -> t g r j", g=RUNS, t=PACK)
         identity = keep.tile([P, P], F32, name="identity")
         make_identity(nc, identity[:])
 
-        def fetch(places, name, t, c0, c1):
-            values = keep.tile([P, c1 - c0], F32, name=f"{name}{t}_{c0}")
-            nc.vector.tensor_tensor(values[:], h_sb[t][:].indirect(entries(places, c0, c1)), h_less[t][:, c0:c1], ALU.add)
-            return values
+        for t in range(1, PACK):
+            take_h(t, 0, S)
+            nc.scalar.activation(h_less[t][:], h_banks[t][:], COPY, scale=OWN_FACTOR * H_FACTOR)
+        nc.scalar.activation(h_less[0][:], h_sb[0][:], COPY, scale=OWN_FACTOR)
 
-        def finish(third, fourth, t, c0, c1):
-            result = keep.tile([P, c1 - c0], F32, name=f"result{t}_{c0}")
-            nc.vector.tensor_tensor(result[:], third[:], fourth[:], ALU.max)
-            nc.sync.dma_start(out_rows[t, :, :, c0:c1], result[:])
-
-        def finish_by_sums(third, rise, t, u):
+        def finish_by_sums(third, rise, u):
             c0, c1 = HALVES[u]
             blocks = [slice(b * P, (b + 1) * P) for b in range((c1 - c0) // P)]
-            gain = keep.tile([P, c1 - c0], F32, name=f"gain{t}_{u}")
+            gain = keep.tile([P, c1 - c0], F32, name=f"gain{u}")
             nc.scalar.activation(gain[:], rise[:], RELU)
-            sum_bank = psum.tile([P, c1 - c0], F32, name=f"sum_bank{t}_{u}", tag=f"bank{2 + u}")
-            terms = (third[:], h_less[t][:, c0:c1], gain[:])
+            sum_bank = psum.tile([P, c1 - c0], F32, name=f"sum_bank{u}", tag=f"bank{2 + u}")
+            terms = (third[:], h_less[0][:, c0:c1], gain[:])
             for block in blocks:
                 for place, term in enumerate(terms):
                     nc.tensor.matmul(
@@ -263,37 +269,40 @@ def tile_picked_denseminmodover_none_p_kernel(
                         start=place == 0,
                         stop=place == len(terms) - 1,
                     )
-            turned = keep.tile([P, c1 - c0], F32, name=f"turned{t}_{u}")
+            turned = keep.tile([P, c1 - c0], F32, name=f"turned{u}")
             nc.scalar.copy(turned[:], sum_bank[:])
-            back_bank = psum.tile([P, c1 - c0], F32, name=f"back_bank{t}_{u}", tag=f"bank{u}")
+            back_bank = psum.tile([P, c1 - c0], F32, name=f"back_bank{u}", tag=f"bank{u}")
             for block in blocks:
                 nc.tensor.transpose(back_bank[:, block], turned[:, block], identity[:])
+            summed = keep.tile([P, c1 - c0], F32, name=f"summed{u}")
+            nc.scalar.copy(summed[:], back_bank[:])
+            nc.scalar.dma_start(out_rows[0, :, :, c0:c1], summed[:])
+
+        thirds = [keep.tile([P, S // 2], F32, name=f"third0_{u}") for u in range(2)]
+        rises = [keep.tile([P, S // 2], F32, name=f"rise{u}") for u in range(2)]
+        for u in range(2):
+            nc.vector.tensor_copy(thirds[u][:], h_sb[0][:].indirect(entries(n3_sb, *HALVES[u])))
+        for u in range(2):
+            nc.vector.tensor_tensor(
+                rises[u][:], h_sb[0][:].indirect(entries(n4_sb, *HALVES[u])), thirds[u][:], ALU.subtract
+            )
+            finish_by_sums(thirds[u], rises[u], u)
+
+        def fetch(places, name, t, c0, c1):
+            values = keep.tile([P, c1 - c0], F32, name=f"{name}{t}_{c0}")
+            nc.vector.tensor_tensor(values[:], h_sb[t][:].indirect(entries(places, c0, c1)), h_less[t][:, c0:c1], ALU.add)
+            return values
+
+        def finish_by_max(third, fourth, t, c0, c1):
             result = keep.tile([P, c1 - c0], F32, name=f"result{t}_{c0}")
-            nc.scalar.copy(result[:], back_bank[:])
-            nc.scalar.dma_start(out_rows[t, :, :, c0:c1], result[:])
+            nc.vector.tensor_tensor(result[:], third[:], fourth[:], ALU.max)
+            nc.sync.dma_start(out_rows[t, :, :, c0:c1], result[:])
 
-        take_h(1, 0, S)
-        for t in (2, 3):
-            take_h(t, 0, S)
-            take_less(t, 0, S)
-        nc.scalar.activation(h_less[0][:], h_sb[0][:], COPY, scale=-0.75)
-        take_less(1, 0, S)
-        for t in (0, 1):
-            thirds = [keep.tile([P, S // 2], F32, name=f"third{t}_{u}") for u in range(2)]
-            rises = [keep.tile([P, S // 2], F32, name=f"rise{t}_{u}") for u in range(2)]
-            for u in range(2):
-                nc.vector.tensor_copy(thirds[u][:], h_sb[t][:].indirect(entries(n3_sb, *HALVES[u])))
-            for u in range(2):
-                nc.vector.tensor_tensor(
-                    rises[u][:], h_sb[t][:].indirect(entries(n4_sb, *HALVES[u])), thirds[u][:], ALU.subtract
-                )
-                finish_by_sums(thirds[u], rises[u], t, u)
-
-        pieces = [(2, c0, c1) for c0, c1 in HALVES] + [(3, c0, c1) for c0, c1 in LAST_PIECES]
+        pieces = [(t, 0, S) for t in WIDE_TILES] + [(PACK - 1, c0, c1) for c0, c1 in LAST_PIECES]
         waiting = None
         for piece in pieces:
             third = fetch(n3_sb, "third", *piece)
             if waiting is not None:
-                finish(*waiting)
+                finish_by_max(*waiting)
             waiting = (third, fetch(n4_sb, "fourth", *piece), *piece)
-        finish(*waiting)
+        finish_by_max(*waiting)

from contextlib import ExitStack

import concourse.mybir as mybir
from concourse.masks import make_identity

K, T, S, H, G = 512, 2048, 512, 512, 2048
FLOPS = 2 * 2 * K * H * S

F32 = mybir.dt.float32
BF16 = mybir.dt.bfloat16
I32 = mybir.dt.int32
U32 = mybir.dt.uint32
U16 = mybir.dt.uint16
U8 = mybir.dt.uint8
FP8X4 = mybir.dt.float8_e4m3fn_x4
ALU = mybir.AluOpType
COPY = mybir.ActivationFunctionType.Copy
RELU = mybir.ActivationFunctionType.Relu

P = 128
PACK = 4
RUNS = 8
QUADRANT = 32
LIST_ROWS = 16
HALVES = ((0, S // 2), (S // 2, S))
QUARTER = S // 4
WIDE_TILES = (1, 2)
LAST_PIECES = ((0, S // 2), (S // 2, 3 * S // 4), (3 * S // 4, S))
H_FACTOR = 0.0625
OWN_FACTOR = -0.75


def tile_picked_denseminmodover_none_p_kernel(
    tc, x_words, x_scales, w1, gs, d_words, d_scales, offs, n1, n2, k1, n3, n4, out
):
    nc = tc.nc
    with ExitStack() as ctx:
        lists = ctx.enter_context(tc.tile_pool(name="lists", bufs=1))
        keep = ctx.enter_context(tc.tile_pool(name="keep", bufs=1))
        psum = ctx.enter_context(tc.psum_pool(name="psum", bufs=1))

        def list_tile(name):
            return lists.tile([P, S // LIST_ROWS], U16, name=name)

        def entries(tile, c0, c1):
            return tile[:, c0 // LIST_ROWS : c1 // LIST_ROWS]

        def gathered_scale_rows(tile, row):
            return tile[LIST_ROWS * (row // 2) + row % 2 : P : QUADRANT]

        offs_sb, n1_sb, n2_sb = list_tile("offs_sb"), list_tile("n1_sb"), list_tile("n2_sb")
        k1_sb, n3_sb, n4_sb = list_tile("k1_sb"), list_tile("n3_sb"), list_tile("n4_sb")

        x_scale_table = keep.tile([P, T], U8, name="x_scale_table")
        d_scale_table = keep.tile([P, G], U8, name="d_scale_table")
        d_scale_rows = keep.tile([P, H], U8, name="d_scale_rows", align_bytes=64)
        x_word_table = keep.tile([P, T], U32, name="x_word_table")
        d_word_table = keep.tile([P, G], U32, name="d_word_table")
        w_raw = [keep.tile([P, PACK, H // 2], F32, name=f"w_raw{u}") for u in range(2)]
        gs_sb = keep.tile([P, PACK], F32, name="gs_sb")

        nc.vector.memset(x_scale_table[:].bitcast(I32), 0)
        nc.vector.memset(d_scale_table[:].bitcast(I32), 0)

        nc.gpsimd.dma_start(gs_sb[:], gs.rearrange("(p t) o -> p (t o)", t=PACK))
        w_rows = w1.rearrange("(p j) c -> p j c", j=PACK)
        nc.sync.dma_start(w_raw[0][:], w_rows[:, :, : H // 2])
        nc.sync.dma_start(offs_sb[:], offs)
        nc.sync.dma_start(w_raw[1][:], w_rows[:, :, H // 2 :])
        for q in range(P // QUADRANT):
            nc.sync.dma_start(
                x_scale_table[QUADRANT * q : QUADRANT * q + 4, :].bitcast(I32),
                x_scales[0, 4 * q : 4 * q + 4, :].bitcast(I32),
            )
        nc.sync.dma_start(x_word_table[:].bitcast(I32), x_words[0].rearrange("p n t -> p (n t)").bitcast(I32))
        nc.sync.dma_start(k1_sb[:], k1)
        d_scales_by_row = d_scales[0].rearrange("(q row) n -> row q n", row=4)
        for row in range(4):
            nc.sync.dma_start(gathered_scale_rows(d_scale_table, row).bitcast(I32), d_scales_by_row[row].bitcast(I32))
        nc.vector.memset(d_scale_rows[:].bitcast(I32), 0)
        nc.sync.dma_start(n1_sb[:], n1)
        nc.sync.dma_start(n2_sb[:], n2)
        nc.sync.dma_start(d_word_table[:].bitcast(I32), d_words[0].rearrange("p n t -> p (n t)").bitcast(I32))
        nc.sync.dma_start(n3_sb[:], n3)
        nc.sync.dma_start(n4_sb[:], n4)

        w_grouped = keep.tile([P, PACK, P, PACK], BF16, name="w_grouped", align_bytes=64)
        for u, copy in enumerate((nc.vector.tensor_copy, nc.scalar.copy)):
            copy(
                w_grouped[:, :, u * (P // 2) : (u + 1) * (P // 2), :].rearrange("p t m j -> p m j t"),
                w_raw[u][:].rearrange("p j (m t) -> p m j t", t=PACK),
            )
        x_scale_picked = keep.tile([P, S], U8, name="x_scale_picked", align_bytes=64)
        x_word_picked = keep.tile([P, S], U32, name="x_word_picked", align_bytes=64)
        nc.vector.tensor_copy(x_scale_picked[:], x_scale_table[:].indirect(offs_sb[:]))
        w_words = [keep.tile([P, P], U32, name=f"w_words{t}", align_bytes=64) for t in range(PACK)]
        w_scales = [keep.tile([P, P], U8, name=f"w_scales{t}", align_bytes=64) for t in range(PACK)]
        for t in range(PACK):
            nc.vector.quantize_mx(
                out=w_words[t][:].bitcast(FP8X4), scales=w_scales[t][:], in_=w_grouped[:, t].rearrange("p m j -> p (m j)")
            )
        for c0, c1 in HALVES:
            nc.vector.tensor_copy(x_word_picked[:, c0:c1], x_word_table[:].indirect(entries(offs_sb, c0, c1)))

        def first_product(t, c0, c1, tag):
            bank = psum.tile([P, c1 - c0], F32, name=f"y_bank{t}_{c0}", tag=tag)
            nc.tensor.matmul_mx(
                out=bank[:],
                lhsT=w_words[t][:].bitcast(FP8X4),
                lhsT_scale=w_scales[t][:],
                rhs=x_word_picked[:, c0:c1].bitcast(FP8X4),
                rhs_scale=x_scale_picked[:, c0:c1],
                start=True,
                stop=True,
            )
            return bank

        y_halves = [[first_product(0, *HALVES[0], "bank7")[:], first_product(0, *HALVES[1], "bank0")[:]]]
        y_banks = {}
        for t in range(1, PACK):
            y_banks[t] = first_product(t, 0, S, f"bank{t}")
            y_halves.append([y_banks[t][:, c0:c1] for c0, c1 in HALVES])

        y_sb = [keep.tile([P, S], F32, name=f"y_sb{t}") for t in range(PACK)]
        h_sb = [keep.tile([P, 2 * S if t in WIDE_TILES else S], F32, name=f"h_sb{t}") for t in range(PACK)]
        own = [h_sb[t][:, S:] if t in WIDE_TILES else keep.tile([P, S], F32, name=f"y_own{t}")[:] for t in range(PACK)]
        y_own = [[own[t][:, c0:c1] for t in range(PACK)] for c0, c1 in HALVES]

        def weighted(target, source, t):
            nc.scalar.activation(target, source, COPY, scale=gs_sb[:, t : t + 1])

        weighted(y_sb[0][:, : S // 2], y_halves[0][0], 0)
        weighted(y_own[0][0], y_halves[0][0], 0)
        weighted(y_sb[0][:, S // 2 :], y_halves[0][1], 0)
        for t in range(1, PACK):
            weighted(y_sb[t][:], y_banks[t][:], t)
            weighted(y_own[0][t], y_halves[t][0], t)
        for t in range(PACK):
            weighted(y_own[1][t], y_halves[t][1], t)

        d_scale_picked = keep.tile([P, H], U8, name="d_scale_picked")
        d_scale_dealt = keep.tile([P, PACK, P], U8, name="d_scale_dealt")
        nc.vector.tensor_copy(d_scale_picked[:], d_scale_table[:].indirect(k1_sb[:]))

        def place_d_scales():
            nc.vector.tensor_copy(
                d_scale_dealt[:].bitcast(I32).rearrange("p t (g w) -> p t g w", g=RUNS),
                d_scale_picked[:].bitcast(I32).rearrange("p (g t w) -> p t g w", g=RUNS, t=PACK),
            )
            for row in range(4):
                nc.sync.dma_start(
                    d_scale_rows[row:P:QUADRANT, :].bitcast(I32),
                    gathered_scale_rows(d_scale_dealt, row).rearrange("p t m -> p (t m)").bitcast(I32),
                )

        pa_neg = [keep.tile([P, PACK, S // 2], F32, name=f"pa_neg{u}") for u in range(2)]
        pb = [keep.tile([P, PACK, S // 2], F32, name=f"pb{u}") for u in range(2)]

        def difference(values, places, t, u):
            nc.vector.tensor_tensor(
                values[u][:, t, :], y_sb[t][:].indirect(entries(places, *HALVES[u])), y_own[u][t], ALU.subtract
            )

        def rounded(values, name, u, func, sign):
            grouped = keep.tile([P, S // 2, PACK], BF16, name=f"{name}_bf{u}")
            nc.scalar.activation(
                grouped[:].rearrange("p (c i) t -> p c t i", i=4),
                values[u][:].rearrange("p t (c i) -> p c t i", i=4),
                func,
                scale=sign,
            )
            return grouped[:].rearrange("p c t -> p (c t)")

        difference(pa_neg, n1_sb, 0, 0)
        place_d_scales()
        difference(pb, n2_sb, 0, 0)
        for t in range(1, PACK):
            difference(pa_neg, n1_sb, t, 0)
            difference(pb, n2_sb, t, 0)

        d_word_picked = keep.tile([P, H], U32, name="d_word_picked")
        d_word_dealt = keep.tile([P, PACK, P], U32, name="d_word_dealt", align_bytes=64)
        nc.vector.tensor_copy(d_word_picked[:], d_word_table[:].indirect(k1_sb[:]))
        for t in range(PACK):
            nc.sync.dma_start(
                d_word_dealt[:, t, :].bitcast(I32).rearrange("p (g r) -> p g r", g=RUNS),
                d_word_picked[:].bitcast(I32).rearrange("p (g t r) -> p t g r", g=RUNS, t=PACK)[:, t],
            )

        pa_bf = [rounded(pa_neg, "pa", 0, COPY, -1.0)]
        pb_bf = [rounded(pb, "pb", 0, COPY, 1.0)]
        high_bf = [rounded(pb, "high", 0, RELU, 1.0)]
        for t in range(PACK):
            difference(pb, n2_sb, t, 1)
        pb_bf.append(rounded(pb, "pb", 1, COPY, 1.0))
        high_bf.append(rounded(pb, "high", 1, RELU, 1.0))
        for t in range(PACK):
            difference(pa_neg, n1_sb, t, 1)
        pa_bf.append(rounded(pa_neg, "pa", 1, COPY, -1.0))

        def quarter(halves, v):
            return halves[v // 2][:, (v % 2) * PACK * QUARTER : (v % 2 + 1) * PACK * QUARTER]

        h_banks = [psum.tile([P, S], F32, name=f"h_bank{t}", tag=f"bank{PACK + t}") for t in range(PACK)]
        h_less = [keep.tile([P, S], F32, name=f"h_less{t}") for t in range(PACK)]
        late_banks = {v: psum.tile([P, QUARTER], F32, name=f"late_bank{v}", tag=f"bank{v - 2}") for v in (2, 3)}

        def h_sums(t, c0, c1):
            v = c0 // QUARTER
            return late_banks[v][:] if t == 0 and v in late_banks else h_banks[t][:, c0:c1]

        def take_h(t, c0, c1):
            nc.scalar.activation(h_sb[t][:, c0:c1], h_sums(t, c0, c1), COPY, scale=H_FACTOR)

        for u in range(2):
            pair = (2 * u, 2 * u + 1)
            low = {v: keep.tile([P, PACK * QUARTER], BF16, name=f"low{v}") for v in pair}
            raised = {v: keep.tile([P, PACK * QUARTER], BF16, name=f"raised{v}") for v in pair}
            z_bf = {v: keep.tile([P, PACK * QUARTER], BF16, name=f"z_bf{v}", align_bytes=64) for v in pair}
            for v in pair:
                nc.vector.tensor_scalar_min(low[v][:], quarter(pb_bf, v), 0.0)
            for v in pair:
                nc.vector.tensor_tensor(raised[v][:], quarter(pa_bf, v), low[v][:], ALU.max)
            for v in pair:
                nc.vector.tensor_tensor(z_bf[v][:], raised[v][:], quarter(high_bf, v), ALU.min)
            for v in pair:
                c0, c1 = v * QUARTER, (v + 1) * QUARTER
                z_words = keep.tile([P, QUARTER], U32, name=f"z_words{v}", align_bytes=64)
                z_scales = keep.tile([P, QUARTER], U8, name=f"z_scales{v}", align_bytes=64)
                nc.vector.quantize_mx(out=z_words[:].bitcast(FP8X4), scales=z_scales[:], in_=z_bf[v][:])
                for t in range(PACK):
                    nc.tensor.matmul_mx(
                        out=h_sums(t, c0, c1),
                        lhsT=d_word_dealt[:, t, :].bitcast(FP8X4),
                        lhsT_scale=d_scale_rows[:, t * P : (t + 1) * P],
                        rhs=z_words[:].bitcast(FP8X4),
                        rhs_scale=z_scales[:],
                        start=True,
                        stop=True,
                    )
                if v in late_banks:
                    take_h(0, c0, c1)
                elif c1 == S // 2:
                    take_h(0, *HALVES[0])

        out_rows = out.rearrange("(g t r) j -> t g r j", g=RUNS, t=PACK)
        identity = keep.tile([P, P], F32, name="identity")
        make_identity(nc, identity[:])

        for t in range(1, PACK):
            take_h(t, 0, S)
            nc.scalar.activation(h_less[t][:], h_banks[t][:], COPY, scale=OWN_FACTOR * H_FACTOR)
        nc.scalar.activation(h_less[0][:], h_sb[0][:], COPY, scale=OWN_FACTOR)

        def finish_by_sums(third, rise, u):
            c0, c1 = HALVES[u]
            blocks = [slice(b * P, (b + 1) * P) for b in range((c1 - c0) // P)]
            gain = keep.tile([P, c1 - c0], F32, name=f"gain{u}")
            nc.scalar.activation(gain[:], rise[:], RELU)
            sum_bank = psum.tile([P, c1 - c0], F32, name=f"sum_bank{u}", tag=f"bank{2 + u}")
            terms = (third[:], h_less[0][:, c0:c1], gain[:])
            for block in blocks:
                for place, term in enumerate(terms):
                    nc.tensor.matmul(
                        sum_bank[:, block],
                        lhsT=term[:, block],
                        rhs=identity[:],
                        is_transpose=True,
                        start=place == 0,
                        stop=place == len(terms) - 1,
                    )
            turned = keep.tile([P, c1 - c0], F32, name=f"turned{u}")
            nc.scalar.copy(turned[:], sum_bank[:])
            back_bank = psum.tile([P, c1 - c0], F32, name=f"back_bank{u}", tag=f"bank{u}")
            for block in blocks:
                nc.tensor.transpose(back_bank[:, block], turned[:, block], identity[:])
            summed = keep.tile([P, c1 - c0], F32, name=f"summed{u}")
            nc.scalar.copy(summed[:], back_bank[:])
            nc.scalar.dma_start(out_rows[0, :, :, c0:c1], summed[:])

        thirds = [keep.tile([P, S // 2], F32, name=f"third0_{u}") for u in range(2)]
        rises = [keep.tile([P, S // 2], F32, name=f"rise{u}") for u in range(2)]
        for u in range(2):
            nc.vector.tensor_copy(thirds[u][:], h_sb[0][:].indirect(entries(n3_sb, *HALVES[u])))
        for u in range(2):
            nc.vector.tensor_tensor(
                rises[u][:], h_sb[0][:].indirect(entries(n4_sb, *HALVES[u])), thirds[u][:], ALU.subtract
            )
            finish_by_sums(thirds[u], rises[u], u)

        def fetch(places, name, t, c0, c1):
            values = keep.tile([P, c1 - c0], F32, name=f"{name}{t}_{c0}")
            nc.vector.tensor_tensor(values[:], h_sb[t][:].indirect(entries(places, c0, c1)), h_less[t][:, c0:c1], ALU.add)
            return values

        def finish_by_max(third, fourth, t, c0, c1):
            result = keep.tile([P, c1 - c0], F32, name=f"result{t}_{c0}")
            nc.vector.tensor_tensor(result[:], third[:], fourth[:], ALU.max)
            nc.sync.dma_start(out_rows[t, :, :, c0:c1], result[:])

        pieces = [(t, 0, S) for t in WIDE_TILES] + [(PACK - 1, c0, c1) for c0, c1 in LAST_PIECES]
        waiting = None
        for piece in pieces:
            third = fetch(n3_sb, "third", *piece)
            if waiting is not None:
                finish_by_max(*waiting)
            waiting = (third, fetch(n4_sb, "fourth", *piece), *piece)
        finish_by_max(*waiting)
